import numpy as np
import ml_dtypes


def mxq(x, axis, fmt="e4m3"):
    dtype, down = {"e4m3": (ml_dtypes.float8_e4m3fn, 7), "e5m2": (ml_dtypes.float8_e5m2, 14)}[fmt]
    v = np.moveaxis(np.asarray(x, np.float32).astype(ml_dtypes.bfloat16).astype(np.float64), axis, -1)
    blocks = v.reshape(v.shape[:-1] + (-1, 32))
    amax = np.abs(blocks).max(-1, keepdims=True)
    byte = np.maximum(np.where(amax > 0, np.frexp(amax)[1] - 1 + 127, 0) - down, 1)
    scale = np.exp2(byte - 127.0)
    codes = (blocks / scale).astype(np.float32).astype(dtype).astype(np.float64)
    return np.moveaxis((codes * scale).reshape(v.shape), -1, axis)


WIDE = False


def mx_kscale(k):
    if not WIDE:
        return np.ones(k)
    levels = np.array([10, -10, 5, -5, 0])
    if k % 512:
        return np.exp2(np.random.permutation(np.resize(levels, k // 32))).repeat(32)
    a = np.empty((k // 512, 16))
    for p in range(k // 512):
        a[p, :8] = np.random.permutation(np.resize(levels, 8))
        for g in range(8):
            far = levels[np.abs(levels - a[p, g]) >= 10]
            a[p, g + 8] = far[np.random.randint(len(far))]
    return np.exp2(a.ravel()).repeat(32)


def f64(x):
    return np.asarray(x).astype(np.float64)


def striped(idx):
    return np.tile(idx.reshape(-1, 16).T, (8, 1)).astype(np.uint16)


def unstriped(offs):
    return offs[:16].T.reshape(-1).astype(np.int64)


def pack_weight(w):
    k, n = w.shape
    w = f64(np.asarray(w, np.float32).astype(ml_dtypes.bfloat16)).reshape(k // 32, 32, n)
    amax = np.abs(w).max(1)
    byte = np.clip(np.where(amax > 0, np.frexp(amax)[1] - 1 + 127 - 7, 1), 1, 254)
    scaled = (w * np.exp2(127.0 - byte)[:, None, :]).reshape(k, n).astype(np.float32)
    words = np.ascontiguousarray(scaled.reshape(k // 512, 128, 4, n).transpose(0, 1, 3, 2)).astype(ml_dtypes.float8_e4m3fn).view(np.uint8)
    return words, np.ascontiguousarray(byte.astype(np.uint8).reshape(k // 512, 16, n))


def unpack_weight(words, scales):
    g, p, n, _ = words.shape
    vals = np.ascontiguousarray(words).view(ml_dtypes.float8_e4m3fn).astype(np.float64) * np.repeat(np.exp2(scales.astype(np.float64) - 127.0), 8, axis=1)[..., None]
    return vals.transpose(0, 1, 3, 2).reshape(g * 512, n)


K, T, S, N = 1024, 1024, 512, 256


def setup_inputs():
    n = np.random.standard_normal
    s = mx_kscale(K)[:, None]
    words, scales = pack_weight(n((K, N)) / np.sqrt(K) / s)
    return {
        "xT": (n((K, T)) * s).astype(np.float32),
        "w_words": words,
        "w_scales": scales,
        "offs": striped(np.sort(np.random.permutation(T)[:S])),
    }


def reference(xT, w_words, w_scales, offs):
    w = unpack_weight(w_words, w_scales)
    idx = unstriped(offs)
    xq = mxq(f64(xT)[:, idx], 0, "e4m3")
    y = w.T @ xq
    return y

@@ -1,0 +1,127 @@
+from contextlib import ExitStack
+
+import concourse.mybir as mybir
+
+K, T, S, N = 1024, 1024, 512, 256
+FLOPS = 2 * K * S * N
+
+F32 = mybir.dt.float32
+BF16 = mybir.dt.bfloat16
+I32 = mybir.dt.int32
+U32 = mybir.dt.uint32
+U16 = mybir.dt.uint16
+U8 = mybir.dt.uint8
+FP8X4 = mybir.dt.float8_e4m3fn_x4
+
+P = 128
+PACK = 4
+K_PASS = P * PACK
+PASSES = K // K_PASS
+HALVES = N // P
+LIST_ROWS = 16
+
+CHUNKS = (
+    ((256, 192), (256, 192), (256, 192), (256, 192)),
+    ((256, 192), (256, 192), (256, 192), (128, 96), (128, 48)),
+)
+SLICES = ((0, 256), (256, 384), (384, 512))
+
+
+def tile_picked_pick_lin_none_srt_e_kernel(tc, xT, w_words, w_scales, offs, out):
+    nc = tc.nc
+    with ExitStack() as ctx:
+        keep = ctx.enter_context(tc.tile_pool(name="keep", bufs=1))
+        psum = ctx.enter_context(tc.psum_pool(name="psum", bufs=1))
+
+        offsets = keep.tile([P, S // LIST_ROWS], U16, name="offsets")
+        w_codes = [keep.tile([P, N], I32, name=f"w_codes{a}", align_bytes=64) for a in range(PASSES)]
+        w_plane = keep.tile([P, PASSES, N], U8, name="w_plane", align_bytes=64)
+        all_codes = [keep.tile([P, T], U32, name=f"all_codes{a}", align_bytes=64) for a in range(PASSES)]
+        all_plane = [keep.tile([P, T], U8, name=f"all_plane{a}", align_bytes=64) for a in range(PASSES)]
+        got_codes = [keep.tile([P, S], U32, name=f"got_codes{a}", align_bytes=64) for a in range(PASSES)]
+        got_plane = [keep.tile([P, S], U8, name=f"got_plane{a}", align_bytes=64) for a in range(PASSES)]
+        acc = {
+            (h, s): psum.tile([P, hi - lo], F32, name=f"acc{h}_{s}")
+            for h in range(HALVES)
+            for s, (lo, hi) in enumerate(SLICES)
+        }
+
+        nc.vector.memset(w_plane[:].rearrange("p a n -> p (a n)").bitcast(I32), 0)
+        for a in range(PASSES):
+            nc.vector.memset(all_plane[a][:].bitcast(I32), 0)
+
+        def load_w(a):
+            nc.sync.dma_start(out=w_codes[a][:], in_=w_words[a].rearrange("p n t -> p (n t)").bitcast(I32))
+
+        raw = {}
+        for a in range(PASSES):
+            rows = xT[a * K_PASS : (a + 1) * K_PASS, :].rearrange("(p j) t -> p j t", j=PACK)
+            t0 = 0
+            for c, (width, unused) in enumerate(CHUNKS[a]):
+                raw[a, c] = keep.tile([P, PACK, width], F32, name=f"raw{a}_{c}")
+                nc.sync.dma_start(out=raw[a, c][:], in_=rows[:, :, t0 : t0 + width])
+                t0 += width
+                if (a, c) == (0, 1):
+                    nc.sync.dma_start(offsets[:], offs)
+                if (a, c) == (1, 0):
+                    load_w(0)
+        load_w(1)
+        for q in range(4):
+            nc.scalar.dma_start(
+                out=w_plane[32 * q : 32 * q + 4, :, :].bitcast(I32),
+                in_=w_scales[:, 4 * q : 4 * q + 4, :].rearrange("a r n -> r a n").bitcast(I32),
+            )
+
+        def rounded(engine_copy, dst, src, lo, hi):
+            engine_copy(
+                out=dst[:, lo:hi, :].rearrange("p (c i) t -> p c t i", i=4),
+                in_=src[:, :, lo:hi].rearrange("p t (c i) -> p c t i", i=4),
+            )
+
+        def gather(a, lo, hi):
+            part = offsets[:, lo // LIST_ROWS : hi // LIST_ROWS]
+            nc.vector.tensor_copy(out=got_plane[a][:, lo:hi], in_=all_plane[a][:].indirect(part))
+            nc.vector.tensor_copy(out=got_codes[a][:, lo:hi], in_=all_codes[a][:].indirect(part))
+
+        def multiply(a, s):
+            lo, hi = SLICES[s]
+            for h in range(HALVES):
+                nc.tensor.matmul_mx(
+                    out=acc[h, s][:],
+                    lhsT=w_codes[a][:, h * P : (h + 1) * P].bitcast(FP8X4),
+                    lhsT_scale=w_plane[:, a, h * P : (h + 1) * P],
+                    rhs=got_codes[a][:, lo:hi].bitcast(FP8X4),
+                    rhs_scale=got_plane[a][:, lo:hi],
+                    start=(a == 0),
+                    stop=(a == PASSES - 1),
+                )
+
+        for a in range(PASSES):
+            t0 = 0
+            for c, (width, share) in enumerate(CHUNKS[a]):
+                grouped = keep.tile([P, width, PACK], BF16, name=f"grouped{a}_{c}", align_bytes=64)
+                rounded(nc.scalar.copy, grouped, raw[a, c], 0, share)
+                rounded(nc.vector.tensor_copy, grouped, raw[a, c], share, width)
+                nc.vector.quantize_mx(
+                    out=all_codes[a][:, t0 : t0 + width].bitcast(FP8X4),
+                    scales=all_plane[a][:, t0 : t0 + width],
+                    in_=grouped[:].rearrange("p w j -> p (w j)"),
+                )
+                t0 += width
+                if a == 1 and c < 2:
+                    gather(0, c * S // 2, (c + 1) * S // 2)
+        for s in range(len(SLICES)):
+            multiply(0, s)
+
+        out_rows = out.rearrange("(h p) j -> p h j", p=P)
+        for s, (lo, hi) in enumerate(SLICES):
+            gather(1, lo, hi)
+            multiply(1, s)
+        for s, (lo, hi) in enumerate(SLICES):
+            result = keep.tile([P, HALVES, hi - lo], F32, name=f"result{s}")
+            nc.scalar.copy(out=result[:, 0, :], in_=acc[0, s][:])
+            if s == len(SLICES) - 1:
+                nc.vector.tensor_copy(out=result[:, 1, :], in_=acc[1, s][:])
+            else:
+                nc.scalar.copy(out=result[:, 1, :], in_=acc[1, s][:])
+            nc.sync.dma_start(out=out_rows[:, :, lo:hi], in_=result[:])

@@ -15,16 +15,17 @@ FP8X4 = mybir.dt.float8_e4m3fn_x4
 
 P = 128
 PACK = 4
+PAIR = 2
 K_PASS = P * PACK
 PASSES = K // K_PASS
 HALVES = N // P
 LIST_ROWS = 16
+SLICE = 128
+SLICES = S // SLICE
 
-CHUNKS = (
-    ((256, 192), (256, 192), (256, 192), (256, 192)),
-    ((256, 192), (256, 192), (256, 192), (128, 96), (128, 48)),
-)
-SLICES = ((0, 256), (256, 384), (384, 512))
+CHUNKS = {(0, 0): ((640, 128), (384, 192)), (0, 1): ((640, 352), (384, 224)), (1, 0): ((256, 256), (512, 352), (256, 256)), (1, 1): ((256, 256), (384, 384), (128, 128), (128, 32), (128, 128))}
+LOADS = ((0, 0, 0), (0, 0, 1), (0, 1, 0), (0, 1, 1), (1, 0, 0), (1, 0, 1), (1, 0, 2), (1, 1, 0), (1, 1, 1), (1, 1, 2), (1, 1, 3), (1, 1, 4))
+PLAN = (('c', 0, 0, 0), ('c', 0, 0, 1), ('g', 0, 0, 0, 128), ('g', 0, 0, 128, 512), ('c', 0, 1, 1), ('c', 0, 1, 0), ('g', 0, 1, 128, 384), ('g', 0, 1, 0, 128), ('i', 0, 0, 256), ('g', 0, 1, 384, 512), ('i', 0, 256, 512), ('c', 1, 0, 0), ('c', 1, 0, 2), ('c', 1, 0, 1), ('c', 1, 1, 2), ('s', 1, 0, 0, 128), ('s', 1, 0, 128, 512), ('q', 0, 0, 512), ('m', 0, 0), ('m', 0, 2), ('m', 0, 1), ('m', 0, 3), ('c', 1, 1, 0), ('c', 1, 1, 1), ('c', 1, 1, 3), ('c', 1, 1, 4), ('s', 1, 1, 0, 128), ('q', 1, 0, 128), ('m', 1, 0), ('s', 1, 1, 128, 384), ('q', 1, 256, 384), ('m', 1, 2), ('s', 1, 1, 384, 512), ('q', 1, 128, 256), ('m', 1, 1), ('q', 1, 384, 512), ('m', 1, 3))
 
 
 def tile_picked_pick_lin_none_srt_e_kernel(tc, xT, w_words, w_scales, offs, out):
@@ -36,92 +37,98 @@ def tile_picked_pick_lin_none_srt_e_kernel(tc, xT, w_words, w_scales, offs, out)
         offsets = keep.tile([P, S // LIST_ROWS], U16, name="offsets")
         w_codes = [keep.tile([P, N], I32, name=f"w_codes{a}", align_bytes=64) for a in range(PASSES)]
         w_plane = keep.tile([P, PASSES, N], U8, name="w_plane", align_bytes=64)
-        all_codes = [keep.tile([P, T], U32, name=f"all_codes{a}", align_bytes=64) for a in range(PASSES)]
-        all_plane = [keep.tile([P, T], U8, name=f"all_plane{a}", align_bytes=64) for a in range(PASSES)]
-        got_codes = [keep.tile([P, S], U32, name=f"got_codes{a}", align_bytes=64) for a in range(PASSES)]
-        got_plane = [keep.tile([P, S], U8, name=f"got_plane{a}", align_bytes=64) for a in range(PASSES)]
+        pairs = {unit: keep.tile([P, T, PAIR], BF16, name=f"pairs{unit[0]}{unit[1]}", align_bytes=64) for unit in CHUNKS}
+        picked = {a: keep.tile([P, PAIR, S], U32, name=f"picked{a}", align_bytes=64) for a in (0,)}
+        grouped = [keep.tile([P, S, PACK], BF16, name=f"grouped{a}", align_bytes=64) for a in range(PASSES)]
+        x_codes = [keep.tile([P, S], U32, name=f"x_codes{a}", align_bytes=64) for a in range(PASSES)]
+        x_plane = [keep.tile([P, S], U8, name=f"x_plane{a}", align_bytes=64) for a in range(PASSES)]
         acc = {
-            (h, s): psum.tile([P, hi - lo], F32, name=f"acc{h}_{s}")
-            for h in range(HALVES)
-            for s, (lo, hi) in enumerate(SLICES)
+            (h, s): psum.tile([P, SLICE], F32, name=f"acc{h}_{s}") for h in range(HALVES) for s in range(SLICES)
         }
 
         nc.vector.memset(w_plane[:].rearrange("p a n -> p (a n)").bitcast(I32), 0)
-        for a in range(PASSES):
-            nc.vector.memset(all_plane[a][:].bitcast(I32), 0)
-
-        def load_w(a):
-            nc.sync.dma_start(out=w_codes[a][:], in_=w_words[a].rearrange("p n t -> p (n t)").bitcast(I32))
 
         raw = {}
-        for a in range(PASSES):
+        for a, u, c in LOADS:
             rows = xT[a * K_PASS : (a + 1) * K_PASS, :].rearrange("(p j) t -> p j t", j=PACK)
-            t0 = 0
-            for c, (width, unused) in enumerate(CHUNKS[a]):
-                raw[a, c] = keep.tile([P, PACK, width], F32, name=f"raw{a}_{c}")
-                nc.sync.dma_start(out=raw[a, c][:], in_=rows[:, :, t0 : t0 + width])
-                t0 += width
-                if (a, c) == (0, 1):
-                    nc.sync.dma_start(offsets[:], offs)
-                if (a, c) == (1, 0):
-                    load_w(0)
-        load_w(1)
+            t0 = sum(width for width, unused in CHUNKS[a, u][:c])
+            width = CHUNKS[a, u][c][0]
+            raw[a, u, c] = keep.tile([P, PAIR, width], F32, name=f"raw{a}{u}_{c}")
+            nc.sync.dma_start(out=raw[a, u, c][:], in_=rows[:, PAIR * u : PAIR * (u + 1), t0 : t0 + width])
+            if (a, u, c) == (0, 0, 0):
+                nc.sync.dma_start(offsets[:], offs)
+        for a in range(PASSES):
+            nc.sync.dma_start(out=w_codes[a][:], in_=w_words[a].rearrange("p n t -> p (n t)").bitcast(I32))
         for q in range(4):
             nc.scalar.dma_start(
                 out=w_plane[32 * q : 32 * q + 4, :, :].bitcast(I32),
                 in_=w_scales[:, 4 * q : 4 * q + 4, :].rearrange("a r n -> r a n").bitcast(I32),
             )
 
-        def rounded(engine_copy, dst, src, lo, hi):
-            engine_copy(
-                out=dst[:, lo:hi, :].rearrange("p (c i) t -> p c t i", i=4),
-                in_=src[:, :, lo:hi].rearrange("p t (c i) -> p c t i", i=4),
+        def round_chunk(a, u, c):
+            t0 = sum(width for width, unused in CHUNKS[a, u][:c])
+            width, share = CHUNKS[a, u][c]
+            src = raw[a, u, c][:].rearrange("p e t -> p t e")
+            if share > 0:
+                nc.scalar.copy(out=pairs[a, u][:, t0 : t0 + share, :], in_=src[:, :share, :])
+            if share < width:
+                nc.vector.tensor_copy(out=pairs[a, u][:, t0 + share : t0 + width, :], in_=src[:, share:, :])
+
+        def grouped_words(a, dtype):
+            return grouped[a][:].rearrange("p j t -> p (j t)").bitcast(dtype).rearrange("p (j u) -> p j u", u=PAIR)
+
+        def gather(a, u, lo, hi, dst):
+            window = pairs[a, u][:].rearrange("p t e -> p (t e)").bitcast(U32)[:, : hi + T - S]
+            nc.vector.tensor_copy(out=dst, in_=window.indirect(offsets[:, lo // LIST_ROWS : hi // LIST_ROWS]))
+
+        def interleave(a, lo, hi):
+            nc.vector.tensor_copy(
+                out=grouped_words(a, I32)[:, lo:hi, :],
+                in_=picked[a][:].bitcast(I32).rearrange("p u j -> p j u")[:, lo:hi, :],
             )
 
-        def gather(a, lo, hi):
-            part = offsets[:, lo // LIST_ROWS : hi // LIST_ROWS]
-            nc.vector.tensor_copy(out=got_plane[a][:, lo:hi], in_=all_plane[a][:].indirect(part))
-            nc.vector.tensor_copy(out=got_codes[a][:, lo:hi], in_=all_codes[a][:].indirect(part))
+        def quantise(a, lo, hi):
+            nc.vector.quantize_mx(
+                out=x_codes[a][:, lo:hi].bitcast(FP8X4),
+                scales=x_plane[a][:, lo:hi],
+                in_=grouped[a][:, lo:hi, :].rearrange("p j t -> p (j t)"),
+            )
 
         def multiply(a, s):
-            lo, hi = SLICES[s]
+            cols = slice(s * SLICE, (s + 1) * SLICE)
             for h in range(HALVES):
                 nc.tensor.matmul_mx(
                     out=acc[h, s][:],
                     lhsT=w_codes[a][:, h * P : (h + 1) * P].bitcast(FP8X4),
                     lhsT_scale=w_plane[:, a, h * P : (h + 1) * P],
-                    rhs=got_codes[a][:, lo:hi].bitcast(FP8X4),
-                    rhs_scale=got_plane[a][:, lo:hi],
+                    rhs=x_codes[a][:, cols].bitcast(FP8X4),
+                    rhs_scale=x_plane[a][:, cols],
                     start=(a == 0),
                     stop=(a == PASSES - 1),
                 )
 
-        for a in range(PASSES):
-            t0 = 0
-            for c, (width, share) in enumerate(CHUNKS[a]):
-                grouped = keep.tile([P, width, PACK], BF16, name=f"grouped{a}_{c}", align_bytes=64)
-                rounded(nc.scalar.copy, grouped, raw[a, c], 0, share)
-                rounded(nc.vector.tensor_copy, grouped, raw[a, c], share, width)
-                nc.vector.quantize_mx(
-                    out=all_codes[a][:, t0 : t0 + width].bitcast(FP8X4),
-                    scales=all_plane[a][:, t0 : t0 + width],
-                    in_=grouped[:].rearrange("p w j -> p (w j)"),
-                )
-                t0 += width
-                if a == 1 and c < 2:
-                    gather(0, c * S // 2, (c + 1) * S // 2)
-        for s in range(len(SLICES)):
-            multiply(0, s)
+        for kind, *args in PLAN:
+            if kind == "c":
+                round_chunk(*args)
+            elif kind == "g":
+                a, u, lo, hi = args
+                gather(a, u, lo, hi, picked[a][:, u, lo:hi])
+            elif kind == "s":
+                a, u, lo, hi = args
+                gather(a, u, lo, hi, grouped_words(a, U32)[:, lo:hi, u])
+            elif kind == "i":
+                interleave(*args)
+            elif kind == "q":
+                quantise(*args)
+            else:
+                multiply(*args)
 
         out_rows = out.rearrange("(h p) j -> p h j", p=P)
-        for s, (lo, hi) in enumerate(SLICES):
-            gather(1, lo, hi)
-            multiply(1, s)
-        for s, (lo, hi) in enumerate(SLICES):
-            result = keep.tile([P, HALVES, hi - lo], F32, name=f"result{s}")
+        for s in range(SLICES):
+            result = keep.tile([P, HALVES, SLICE], F32, name=f"result{s}")
             nc.scalar.copy(out=result[:, 0, :], in_=acc[0, s][:])
-            if s == len(SLICES) - 1:
+            if s == SLICES - 1:
                 nc.vector.tensor_copy(out=result[:, 1, :], in_=acc[1, s][:])
             else:
                 nc.scalar.copy(out=result[:, 1, :], in_=acc[1, s][:])
-            nc.sync.dma_start(out=out_rows[:, :, lo:hi], in_=result[:])
+            nc.sync.dma_start(out=out_rows[:, :, s * SLICE : (s + 1) * SLICE], in_=result[:])

@@ -23,9 +23,10 @@ LIST_ROWS = 16
 SLICE = 128
 SLICES = S // SLICE
 
-CHUNKS = {(0, 0): ((640, 128), (384, 192)), (0, 1): ((640, 352), (384, 224)), (1, 0): ((256, 256), (512, 352), (256, 256)), (1, 1): ((256, 256), (384, 384), (128, 128), (128, 32), (128, 128))}
-LOADS = ((0, 0, 0), (0, 0, 1), (0, 1, 0), (0, 1, 1), (1, 0, 0), (1, 0, 1), (1, 0, 2), (1, 1, 0), (1, 1, 1), (1, 1, 2), (1, 1, 3), (1, 1, 4))
-PLAN = (('c', 0, 0, 0), ('c', 0, 0, 1), ('g', 0, 0, 0, 128), ('g', 0, 0, 128, 512), ('c', 0, 1, 1), ('c', 0, 1, 0), ('g', 0, 1, 128, 384), ('g', 0, 1, 0, 128), ('i', 0, 0, 256), ('g', 0, 1, 384, 512), ('i', 0, 256, 512), ('c', 1, 0, 0), ('c', 1, 0, 2), ('c', 1, 0, 1), ('c', 1, 1, 2), ('s', 1, 0, 0, 128), ('s', 1, 0, 128, 512), ('q', 0, 0, 512), ('m', 0, 0), ('m', 0, 2), ('m', 0, 1), ('m', 0, 3), ('c', 1, 1, 0), ('c', 1, 1, 1), ('c', 1, 1, 3), ('c', 1, 1, 4), ('s', 1, 1, 0, 128), ('q', 1, 0, 128), ('m', 1, 0), ('s', 1, 1, 128, 384), ('q', 1, 256, 384), ('m', 1, 2), ('s', 1, 1, 384, 512), ('q', 1, 128, 256), ('m', 1, 1), ('q', 1, 384, 512), ('m', 1, 3))
+CHUNKS = {(0, 0): ((640, 320), (384, 192)), (0, 1): ((640, 288), (384, 192)), (1, 0): ((512, 512), (512, 320)), (1, 1): ((320, 320), (320, 320), (128, 128), (128, 128), (128, 128))}
+OUT_ENGINES = 'AAAVVAVA'
+LOADS = ((0, 0, 0), (0, 0, 1), (0, 1, 0), (0, 1, 1), (1, 0, 0), (1, 0, 1), (1, 1, 0), (1, 1, 1), (1, 1, 2), (1, 1, 3), (0, 'w', 0), (1, 1, 4), (1, 'w', 0))
+PLAN = (('c', 0, 0, 0), ('c', 0, 0, 1), ('g', 0, 0, 128, 512), ('c', 0, 1, 0), ('g', 0, 0, 0, 128), ('c', 0, 1, 1), ('g', 0, 1, 0, 128), ('i', 0, 0, 128), ('c', 1, 0, 0), ('c', 1, 0, 1), ('s', 1, 0, 0, 512), ('g', 0, 1, 128, 512), ('i', 0, 128, 512), ('q', 0, 0, 512), ('m', 0, 0), ('m', 0, 1), ('m', 0, 2), ('m', 0, 3), ('c', 1, 1, 2), ('c', 1, 1, 0), ('c', 1, 1, 1), ('c', 1, 1, 3), ('c', 1, 1, 4), ('s', 1, 1, 0, 128), ('q', 1, 0, 128), ('m', 1, 0), ('s', 1, 1, 256, 384), ('s', 1, 1, 128, 256), ('q', 1, 128, 256), ('m', 1, 1), ('s', 1, 1, 384, 512), ('q', 1, 384, 512), ('m', 1, 3), ('q', 1, 256, 384), ('m', 1, 2))
 
 
 def tile_picked_pick_lin_none_srt_e_kernel(tc, xT, w_words, w_scales, offs, out):
@@ -35,7 +36,7 @@ def tile_picked_pick_lin_none_srt_e_kernel(tc, xT, w_words, w_scales, offs, out)
         psum = ctx.enter_context(tc.psum_pool(name="psum", bufs=1))
 
         offsets = keep.tile([P, S // LIST_ROWS], U16, name="offsets")
-        w_codes = [keep.tile([P, N], I32, name=f"w_codes{a}", align_bytes=64) for a in range(PASSES)]
+        w_codes = keep.tile([P, PASSES, N], I32, name="w_codes", align_bytes=64)
         w_plane = keep.tile([P, PASSES, N], U8, name="w_plane", align_bytes=64)
         pairs = {unit: keep.tile([P, T, PAIR], BF16, name=f"pairs{unit[0]}{unit[1]}", align_bytes=64) for unit in CHUNKS}
         picked = {a: keep.tile([P, PAIR, S], U32, name=f"picked{a}", align_bytes=64) for a in (0,)}
@@ -46,21 +47,28 @@ def tile_picked_pick_lin_none_srt_e_kernel(tc, xT, w_words, w_scales, offs, out)
             (h, s): psum.tile([P, SLICE], F32, name=f"acc{h}_{s}") for h in range(HALVES) for s in range(SLICES)
         }
 
-        nc.vector.memset(w_plane[:].rearrange("p a n -> p (a n)").bitcast(I32), 0)
+        nc.gpsimd.memset(w_plane[:].rearrange("p a n -> p (a n)").bitcast(I32), 0)
 
         raw = {}
+        def load_w(a):
+            nc.sync.dma_start(out=w_codes[:, a, :], in_=w_words[a].rearrange("p n t -> p (n t)").bitcast(I32))
+
         for a, u, c in LOADS:
+            if u == "w":
+                load_w(a)
+                continue
+            if u == "W":
+                nc.sync.dma_start(out=w_codes[:], in_=w_words.rearrange("a p n t -> p a (n t)").bitcast(I32))
+                continue
             rows = xT[a * K_PASS : (a + 1) * K_PASS, :].rearrange("(p j) t -> p j t", j=PACK)
             t0 = sum(width for width, unused in CHUNKS[a, u][:c])
             width = CHUNKS[a, u][c][0]
             raw[a, u, c] = keep.tile([P, PAIR, width], F32, name=f"raw{a}{u}_{c}")
             nc.sync.dma_start(out=raw[a, u, c][:], in_=rows[:, PAIR * u : PAIR * (u + 1), t0 : t0 + width])
-            if (a, u, c) == (0, 0, 0):
+            if (a, u, c) == LOADS[0]:
                 nc.sync.dma_start(offsets[:], offs)
-        for a in range(PASSES):
-            nc.sync.dma_start(out=w_codes[a][:], in_=w_words[a].rearrange("p n t -> p (n t)").bitcast(I32))
         for q in range(4):
-            nc.scalar.dma_start(
+            nc.gpsimd.dma_start(
                 out=w_plane[32 * q : 32 * q + 4, :, :].bitcast(I32),
                 in_=w_scales[:, 4 * q : 4 * q + 4, :].rearrange("a r n -> r a n").bitcast(I32),
             )
@@ -99,7 +107,7 @@ def tile_picked_pick_lin_none_srt_e_kernel(tc, xT, w_words, w_scales, offs, out)
             for h in range(HALVES):
                 nc.tensor.matmul_mx(
                     out=acc[h, s][:],
-                    lhsT=w_codes[a][:, h * P : (h + 1) * P].bitcast(FP8X4),
+                    lhsT=w_codes[:, a, h * P : (h + 1) * P].bitcast(FP8X4),
                     lhsT_scale=w_plane[:, a, h * P : (h + 1) * P],
                     rhs=x_codes[a][:, cols].bitcast(FP8X4),
                     rhs_scale=x_plane[a][:, cols],
@@ -126,9 +134,7 @@ def tile_picked_pick_lin_none_srt_e_kernel(tc, xT, w_words, w_scales, offs, out)
         out_rows = out.rearrange("(h p) j -> p h j", p=P)
         for s in range(SLICES):
             result = keep.tile([P, HALVES, SLICE], F32, name=f"result{s}")
-            nc.scalar.copy(out=result[:, 0, :], in_=acc[0, s][:])
-            if s == SLICES - 1:
-                nc.vector.tensor_copy(out=result[:, 1, :], in_=acc[1, s][:])
-            else:
-                nc.scalar.copy(out=result[:, 1, :], in_=acc[1, s][:])
+            for h in range(HALVES):
+                copy_out = nc.scalar.copy if OUT_ENGINES[HALVES * s + h] == "A" else nc.vector.tensor_copy
+                copy_out(out=result[:, h, :], in_=acc[h, s][:])
             nc.sync.dma_start(out=out_rows[:, :, s * SLICE : (s + 1) * SLICE], in_=result[:])

@@ -23,10 +23,10 @@ LIST_ROWS = 16
 SLICE = 128
 SLICES = S // SLICE
 
-CHUNKS = {(0, 0): ((640, 320), (384, 192)), (0, 1): ((640, 288), (384, 192)), (1, 0): ((512, 512), (512, 320)), (1, 1): ((320, 320), (320, 320), (128, 128), (128, 128), (128, 128))}
-OUT_ENGINES = 'AAAVVAVA'
-LOADS = ((0, 0, 0), (0, 0, 1), (0, 1, 0), (0, 1, 1), (1, 0, 0), (1, 0, 1), (1, 1, 0), (1, 1, 1), (1, 1, 2), (1, 1, 3), (0, 'w', 0), (1, 1, 4), (1, 'w', 0))
-PLAN = (('c', 0, 0, 0), ('c', 0, 0, 1), ('g', 0, 0, 128, 512), ('c', 0, 1, 0), ('g', 0, 0, 0, 128), ('c', 0, 1, 1), ('g', 0, 1, 0, 128), ('i', 0, 0, 128), ('c', 1, 0, 0), ('c', 1, 0, 1), ('s', 1, 0, 0, 512), ('g', 0, 1, 128, 512), ('i', 0, 128, 512), ('q', 0, 0, 512), ('m', 0, 0), ('m', 0, 1), ('m', 0, 2), ('m', 0, 3), ('c', 1, 1, 2), ('c', 1, 1, 0), ('c', 1, 1, 1), ('c', 1, 1, 3), ('c', 1, 1, 4), ('s', 1, 1, 0, 128), ('q', 1, 0, 128), ('m', 1, 0), ('s', 1, 1, 256, 384), ('s', 1, 1, 128, 256), ('q', 1, 128, 256), ('m', 1, 1), ('s', 1, 1, 384, 512), ('q', 1, 384, 512), ('m', 1, 3), ('q', 1, 256, 384), ('m', 1, 2))
+CHUNKS = {(0, 0): ((640, 320), (384, 224)), (0, 1): ((768, 256), (256, 256)), (1, 0): ((384, 320), (640, 384)), (1, 1): ((384, 384), (384, 288), (256, 256))}
+OUT_ENGINES = 'AAVAVAVA'
+LOADS = ((0, 0, 0), (0, 0, 1), (0, 1, 0), (0, 1, 1), (1, 0, 0), (1, 0, 1), (1, 1, 0), (1, 1, 1), (1, 1, 2), (0, 'w', 0), (1, 'w', 0))
+PLAN = (('c', 0, 0, 0), ('c', 0, 0, 1), ('g', 0, 0, 0, 128), ('g', 0, 0, 128, 512), ('c', 0, 1, 0), ('c', 0, 1, 1), ('g', 0, 1, 0, 256), ('ia', 0, 0, 256), ('g', 0, 1, 256, 512), ('i', 0, 256, 512), ('q', 0, 0, 512), ('m', 0, 0), ('m', 0, 1), ('m', 0, 2), ('m', 0, 3), ('c', 1, 0, 0), ('c', 1, 0, 1), ('g', 1, 0, 0, 512), ('c', 1, 1, 0), ('c', 1, 1, 1), ('c', 1, 1, 2), ('g', 1, 1, 0, 256), ('ia', 1, 0, 128), ('q', 1, 0, 128), ('m', 1, 0), ('ia', 1, 128, 256), ('q', 1, 128, 256), ('m', 1, 1), ('g', 1, 1, 256, 512), ('ia', 1, 256, 384), ('q', 1, 256, 384), ('m', 1, 2), ('ia', 1, 384, 512), ('q', 1, 384, 512), ('m', 1, 3))
 
 
 def tile_picked_pick_lin_none_srt_e_kernel(tc, xT, w_words, w_scales, offs, out):
@@ -39,7 +39,7 @@ def tile_picked_pick_lin_none_srt_e_kernel(tc, xT, w_words, w_scales, offs, out)
         w_codes = keep.tile([P, PASSES, N], I32, name="w_codes", align_bytes=64)
         w_plane = keep.tile([P, PASSES, N], U8, name="w_plane", align_bytes=64)
         pairs = {unit: keep.tile([P, T, PAIR], BF16, name=f"pairs{unit[0]}{unit[1]}", align_bytes=64) for unit in CHUNKS}
-        picked = {a: keep.tile([P, PAIR, S], U32, name=f"picked{a}", align_bytes=64) for a in (0,)}
+        picked = {a: keep.tile([P, PAIR, S], U32, name=f"picked{a}", align_bytes=64) for a in (0, 1)}
         grouped = [keep.tile([P, S, PACK], BF16, name=f"grouped{a}", align_bytes=64) for a in range(PASSES)]
         x_codes = [keep.tile([P, S], U32, name=f"x_codes{a}", align_bytes=64) for a in range(PASSES)]
         x_plane = [keep.tile([P, S], U8, name=f"x_plane{a}", align_bytes=64) for a in range(PASSES)]
@@ -126,6 +126,12 @@ def tile_picked_pick_lin_none_srt_e_kernel(tc, xT, w_words, w_scales, offs, out)
                 gather(a, u, lo, hi, grouped_words(a, U32)[:, lo:hi, u])
             elif kind == "i":
                 interleave(*args)
+            elif kind == "ia":
+                a, lo, hi = args
+                nc.scalar.copy(
+                    out=grouped_words(a, F32)[:, lo:hi, :],
+                    in_=picked[a][:].bitcast(F32).rearrange("p u j -> p j u")[:, lo:hi, :],
+                )
             elif kind == "q":
                 quantise(*args)
             else:

from contextlib import ExitStack

import concourse.mybir as mybir

K, T, S, N = 1024, 1024, 512, 256
FLOPS = 2 * K * S * N

F32 = mybir.dt.float32
BF16 = mybir.dt.bfloat16
I32 = mybir.dt.int32
U32 = mybir.dt.uint32
U16 = mybir.dt.uint16
U8 = mybir.dt.uint8
FP8X4 = mybir.dt.float8_e4m3fn_x4

P = 128
PACK = 4
PAIR = 2
K_PASS = P * PACK
PASSES = K // K_PASS
HALVES = N // P
LIST_ROWS = 16
SLICE = 128
SLICES = S // SLICE

CHUNKS = {(0, 0): ((640, 320), (384, 224)), (0, 1): ((768, 256), (256, 256)), (1, 0): ((384, 320), (640, 384)), (1, 1): ((384, 384), (384, 288), (256, 256))}
OUT_ENGINES = 'AAVAVAVA'
LOADS = ((0, 0, 0), (0, 0, 1), (0, 1, 0), (0, 1, 1), (1, 0, 0), (1, 0, 1), (1, 1, 0), (1, 1, 1), (1, 1, 2), (0, 'w', 0), (1, 'w', 0))
PLAN = (('c', 0, 0, 0), ('c', 0, 0, 1), ('g', 0, 0, 0, 128), ('g', 0, 0, 128, 512), ('c', 0, 1, 0), ('c', 0, 1, 1), ('g', 0, 1, 0, 256), ('ia', 0, 0, 256), ('g', 0, 1, 256, 512), ('i', 0, 256, 512), ('q', 0, 0, 512), ('m', 0, 0), ('m', 0, 1), ('m', 0, 2), ('m', 0, 3), ('c', 1, 0, 0), ('c', 1, 0, 1), ('g', 1, 0, 0, 512), ('c', 1, 1, 0), ('c', 1, 1, 1), ('c', 1, 1, 2), ('g', 1, 1, 0, 256), ('ia', 1, 0, 128), ('q', 1, 0, 128), ('m', 1, 0), ('ia', 1, 128, 256), ('q', 1, 128, 256), ('m', 1, 1), ('g', 1, 1, 256, 512), ('ia', 1, 256, 384), ('q', 1, 256, 384), ('m', 1, 2), ('ia', 1, 384, 512), ('q', 1, 384, 512), ('m', 1, 3))


def tile_picked_pick_lin_none_srt_e_kernel(tc, xT, w_words, w_scales, offs, out):
    nc = tc.nc
    with ExitStack() as ctx:
        keep = ctx.enter_context(tc.tile_pool(name="keep", bufs=1))
        psum = ctx.enter_context(tc.psum_pool(name="psum", bufs=1))

        offsets = keep.tile([P, S // LIST_ROWS], U16, name="offsets")
        w_codes = keep.tile([P, PASSES, N], I32, name="w_codes", align_bytes=64)
        w_plane = keep.tile([P, PASSES, N], U8, name="w_plane", align_bytes=64)
        pairs = {unit: keep.tile([P, T, PAIR], BF16, name=f"pairs{unit[0]}{unit[1]}", align_bytes=64) for unit in CHUNKS}
        picked = {a: keep.tile([P, PAIR, S], U32, name=f"picked{a}", align_bytes=64) for a in (0, 1)}
        grouped = [keep.tile([P, S, PACK], BF16, name=f"grouped{a}", align_bytes=64) for a in range(PASSES)]
        x_codes = [keep.tile([P, S], U32, name=f"x_codes{a}", align_bytes=64) for a in range(PASSES)]
        x_plane = [keep.tile([P, S], U8, name=f"x_plane{a}", align_bytes=64) for a in range(PASSES)]
        acc = {
            (h, s): psum.tile([P, SLICE], F32, name=f"acc{h}_{s}") for h in range(HALVES) for s in range(SLICES)
        }

        nc.gpsimd.memset(w_plane[:].rearrange("p a n -> p (a n)").bitcast(I32), 0)

        raw = {}
        def load_w(a):
            nc.sync.dma_start(out=w_codes[:, a, :], in_=w_words[a].rearrange("p n t -> p (n t)").bitcast(I32))

        for a, u, c in LOADS:
            if u == "w":
                load_w(a)
                continue
            if u == "W":
                nc.sync.dma_start(out=w_codes[:], in_=w_words.rearrange("a p n t -> p a (n t)").bitcast(I32))
                continue
            rows = xT[a * K_PASS : (a + 1) * K_PASS, :].rearrange("(p j) t -> p j t", j=PACK)
            t0 = sum(width for width, unused in CHUNKS[a, u][:c])
            width = CHUNKS[a, u][c][0]
            raw[a, u, c] = keep.tile([P, PAIR, width], F32, name=f"raw{a}{u}_{c}")
            nc.sync.dma_start(out=raw[a, u, c][:], in_=rows[:, PAIR * u : PAIR * (u + 1), t0 : t0 + width])
            if (a, u, c) == LOADS[0]:
                nc.sync.dma_start(offsets[:], offs)
        for q in range(4):
            nc.gpsimd.dma_start(
                out=w_plane[32 * q : 32 * q + 4, :, :].bitcast(I32),
                in_=w_scales[:, 4 * q : 4 * q + 4, :].rearrange("a r n -> r a n").bitcast(I32),
            )

        def round_chunk(a, u, c):
            t0 = sum(width for width, unused in CHUNKS[a, u][:c])
            width, share = CHUNKS[a, u][c]
            src = raw[a, u, c][:].rearrange("p e t -> p t e")
            if share > 0:
                nc.scalar.copy(out=pairs[a, u][:, t0 : t0 + share, :], in_=src[:, :share, :])
            if share < width:
                nc.vector.tensor_copy(out=pairs[a, u][:, t0 + share : t0 + width, :], in_=src[:, share:, :])

        def grouped_words(a, dtype):
            return grouped[a][:].rearrange("p j t -> p (j t)").bitcast(dtype).rearrange("p (j u) -> p j u", u=PAIR)

        def gather(a, u, lo, hi, dst):
            window = pairs[a, u][:].rearrange("p t e -> p (t e)").bitcast(U32)[:, : hi + T - S]
            nc.vector.tensor_copy(out=dst, in_=window.indirect(offsets[:, lo // LIST_ROWS : hi // LIST_ROWS]))

        def interleave(a, lo, hi):
            nc.vector.tensor_copy(
                out=grouped_words(a, I32)[:, lo:hi, :],
                in_=picked[a][:].bitcast(I32).rearrange("p u j -> p j u")[:, lo:hi, :],
            )

        def quantise(a, lo, hi):
            nc.vector.quantize_mx(
                out=x_codes[a][:, lo:hi].bitcast(FP8X4),
                scales=x_plane[a][:, lo:hi],
                in_=grouped[a][:, lo:hi, :].rearrange("p j t -> p (j t)"),
            )

        def multiply(a, s):
            cols = slice(s * SLICE, (s + 1) * SLICE)
            for h in range(HALVES):
                nc.tensor.matmul_mx(
                    out=acc[h, s][:],
                    lhsT=w_codes[:, a, h * P : (h + 1) * P].bitcast(FP8X4),
                    lhsT_scale=w_plane[:, a, h * P : (h + 1) * P],
                    rhs=x_codes[a][:, cols].bitcast(FP8X4),
                    rhs_scale=x_plane[a][:, cols],
                    start=(a == 0),
                    stop=(a == PASSES - 1),
                )

        for kind, *args in PLAN:
            if kind == "c":
                round_chunk(*args)
            elif kind == "g":
                a, u, lo, hi = args
                gather(a, u, lo, hi, picked[a][:, u, lo:hi])
            elif kind == "s":
                a, u, lo, hi = args
                gather(a, u, lo, hi, grouped_words(a, U32)[:, lo:hi, u])
            elif kind == "i":
                interleave(*args)
            elif kind == "ia":
                a, lo, hi = args
                nc.scalar.copy(
                    out=grouped_words(a, F32)[:, lo:hi, :],
                    in_=picked[a][:].bitcast(F32).rearrange("p u j -> p j u")[:, lo:hi, :],
                )
            elif kind == "q":
                quantise(*args)
            else:
                multiply(*args)

        out_rows = out.rearrange("(h p) j -> p h j", p=P)
        for s in range(SLICES):
            result = keep.tile([P, HALVES, SLICE], F32, name=f"result{s}")
            for h in range(HALVES):
                copy_out = nc.scalar.copy if OUT_ENGINES[HALVES * s + h] == "A" else nc.vector.tensor_copy
                copy_out(out=result[:, h, :], in_=acc[h, s][:])
            nc.sync.dma_start(out=out_rows[:, :, s * SLICE : (s + 1) * SLICE], in_=result[:])
